import numpy as np
import ml_dtypes


def mxq(x, axis, fmt="e4m3"):
    dtype, down = {"e4m3": (ml_dtypes.float8_e4m3fn, 7), "e5m2": (ml_dtypes.float8_e5m2, 14)}[fmt]
    v = np.moveaxis(np.asarray(x, np.float32).astype(ml_dtypes.bfloat16).astype(np.float64), axis, -1)
    blocks = v.reshape(v.shape[:-1] + (-1, 32))
    amax = np.abs(blocks).max(-1, keepdims=True)
    byte = np.maximum(np.where(amax > 0, np.frexp(amax)[1] - 1 + 127, 0) - down, 1)
    scale = np.exp2(byte - 127.0)
    codes = (blocks / scale).astype(np.float32).astype(dtype).astype(np.float64)
    return np.moveaxis((codes * scale).reshape(v.shape), -1, axis)


WIDE = False


def mx_kscale(k):
    if not WIDE:
        return np.ones(k)
    levels = np.array([10, -10, 5, -5, 0])
    if k % 512:
        return np.exp2(np.random.permutation(np.resize(levels, k // 32))).repeat(32)
    a = np.empty((k // 512, 16))
    for p in range(k // 512):
        a[p, :8] = np.random.permutation(np.resize(levels, 8))
        for g in range(8):
            far = levels[np.abs(levels - a[p, g]) >= 10]
            a[p, g + 8] = far[np.random.randint(len(far))]
    return np.exp2(a.ravel()).repeat(32)


def f64(x):
    return np.asarray(x).astype(np.float64)


def striped(idx):
    return np.tile(idx.reshape(-1, 16).T, (8, 1)).astype(np.uint16)


def unstriped(offs):
    return offs[:16].T.reshape(-1).astype(np.int64)


K, T, E, C, N = 1536, 1280, 4, 256, 512
M = 384


def by_expert(wq, xq):
    return np.concatenate([wq[e].T @ xq[:, e * C:(e + 1) * C] for e in range(E)], axis=1)


def setup_inputs():
    n = np.random.standard_normal
    s = mx_kscale(K)[:, None]
    v = mx_kscale(N)
    return {
        "xT": (n((K, T)) * s).astype(np.float32),
        "w": (n((E, K, N)) / np.sqrt(K) / s[None] * v[None, None, :]).astype(np.float32),
        "wp": (n((N, M)) / np.sqrt(N) / v[:, None]).astype(np.float32),
        "gate": np.tile(np.random.uniform(0.2, 1.0, E * C), (N, 1)).astype(np.float32),
        "offs": striped(np.random.permutation(T)[:E * C]),
    }


def reference(xT, w, wp, gate, offs):
    idx = unstriped(offs)
    xq = mxq(f64(xT)[:, idx], 0, "e4m3")
    y = by_expert(mxq(f64(w), 1, "e4m3"), xq)
    c = np.zeros((N, T))
    c[:, idx] = f64(gate) * y
    return mxq(f64(wp), 0, "e4m3").T @ mxq(c, 0, "e4m3")

@@ -1,0 +1,322 @@
+from contextlib import ExitStack
+
+import concourse.mybir as mybir
+
+K, T, E, C, N, M = 1536, 1280, 4, 256, 512, 384
+S = E * C
+
+FLOPS = 2 * S * K * N + 2 * S * N * M
+BYTES = 4 * (K * T + E * K * N + N * M + S + M * T) + 2 * S
+
+F32 = mybir.dt.float32
+BF16 = mybir.dt.bfloat16
+U32 = mybir.dt.uint32
+U16 = mybir.dt.uint16
+U8 = mybir.dt.uint8
+FP8X4 = mybir.dt.float8_e4m3fn_x4
+COPY = mybir.ActivationFunctionType.Copy
+MULT = mybir.AluOpType.mult
+ADD = mybir.AluOpType.add
+
+P = 128
+PACK = 4
+K_PASS = P * PACK
+PASSES = K // K_PASS
+HALF = 128
+AHEAD = 6
+WG = 6
+SMB = 2
+X_CHUNKS = (((0, 512), (512, 1280)), ((0, 512), (512, 1280)), ((0, 512), (512, 1280)))
+X_UNITS = ((0, 256), (256, 512), (512, 768), (768, 1024), (1024, 1280))
+X_QUANTS = ((0, 512), (512, 1024), (1024, 1280))
+X_ENGINES = ('SSVSV', 'VSVSS', 'SVVSV')
+W_ENGINES = ('SSSS', 'SSSS', 'SSSS', 'SSSV', 'SVSV', 'SVSV', 'SSSS', 'SSSS', 'SVSV', 'SSSS', 'SSSV', 'SSSS')
+Q_FULL = (False, False, True, True, False, False, False, True, True, True, True, False)
+C_ENGINES = ('SS', 'SS', 'SS', 'SS')
+GATHERS = ((0, 1), (2, 3))
+STEPS = (
+    ('lx', 0, 0),
+    ('lx', 0, 1),
+    ('lx', 1, 0),
+    ('lx', 1, 1),
+    ('lx', 2, 0),
+    ('lx', 2, 1),
+    ('lw', 0),
+    ('lw', 1),
+    ('lw', 2),
+    ('lg',),
+    ('lwp',),
+    ('lw', 3),
+    ('lw', 4),
+    ('lw', 5),
+    ('ix', 0),
+    ('iw', 0),
+    ('qw', 0),
+    ('lw', 6),
+    ('ix', 1),
+    ('ix', 2),
+    ('gw', 0, 0),
+    ('gw', 1, 0),
+    ('gw', 2, 0),
+    ('gb', 0),
+    ('wpq',),
+    ('iw', 1),
+    ('qw', 1),
+    ('lw', 7),
+    ('iw', 2),
+    ('qw', 2),
+    ('lw', 8),
+    ('mm', 0),
+    ('ga', 0),
+    ('qc', 0),
+    ('iw', 3),
+    ('qw', 3),
+    ('lw', 9),
+    ('iw', 4),
+    ('qw', 4),
+    ('lw', 10),
+    ('cp', 0),
+    ('iw', 5),
+    ('qw', 5),
+    ('lw', 11),
+    ('mm', 1),
+    ('ga', 1),
+    ('qc', 1),
+    ('gw', 0, 1),
+    ('gw', 1, 1),
+    ('gw', 2, 1),
+    ('gb', 1),
+    ('iw', 6),
+    ('qw', 6),
+    ('iw', 7),
+    ('qw', 7),
+    ('sc', 0),
+    ('iw', 8),
+    ('qw', 8),
+    ('mm', 2),
+    ('ga', 2),
+    ('qc', 2),
+    ('iw', 9),
+    ('qw', 9),
+    ('iw', 10),
+    ('qw', 10),
+    ('cp', 1),
+    ('sc', 1),
+    ('iw', 11),
+    ('qw', 11),
+    ('mm', 3),
+    ('ga', 3),
+    ('qc', 3),
+    ('cp', 2),
+    ('sc', 2),
+    ('cp', 3),
+    ('sc', 3),
+    ('st',),
+)
+
+def copy_on(nc, engine, out, in_):
+    if engine == "S":
+        nc.scalar.activation(out=out, in_=in_, func=COPY)
+    elif engine == "P":
+        nc.gpsimd.tensor_scalar(out=out, in0=in_, scalar1=1.0, scalar2=0.0, op0=MULT, op1=ADD)
+    else:
+        nc.vector.tensor_copy(out=out, in_=in_)
+
+
+def tile_moe_nxt_lin_none_kernel(tc, xT, w, wp, gate, offs, out):
+    nc = tc.nc
+    with ExitStack() as ctx:
+        held = ctx.enter_context(tc.tile_pool(name="held", bufs=1))
+        xstage = ctx.enter_context(tc.tile_pool(name="xstage", bufs=2))
+        wstage = ctx.enter_context(tc.tile_pool(name="wstage", bufs=AHEAD))
+        wgroup = ctx.enter_context(tc.tile_pool(name="wgroup", bufs=WG))
+        wcodes = ctx.enter_context(tc.tile_pool(name="wcodes", bufs=E * PASSES))
+        small = ctx.enter_context(tc.tile_pool(name="small", bufs=SMB))
+        ypsum = ctx.enter_context(tc.psum_pool(name="ypsum", bufs=4))
+        opsum = ctx.enter_context(tc.psum_pool(name="opsum", bufs=4))
+
+        offsets = held.tile([P, S // 16], U16, name="offsets")
+        gates = held.tile([P, S], F32, name="gates")
+        x_codes = [held.tile([P, T], U32, name=f"x_codes{a}", align_bytes=64) for a in range(PASSES)]
+        x_scales = held.tile([P, T], U8, name="x_scales", align_bytes=64)
+        slot_codes = [held.tile([P, S], U32, name=f"slot_codes{a}", align_bytes=64) for a in range(PASSES)]
+        slot_scales = held.tile([P, S], U8, name="slot_scales", align_bytes=64)
+        wp_raw = held.tile([P, PACK, M], F32, name="wp_raw")
+        wp_grouped = held.tile([P, M * PACK], BF16, name="wp_grouped", align_bytes=64)
+        wp_codes = held.tile([P, M], U32, name="wp_codes", align_bytes=64)
+        wp_scales = held.tile([P, M], U8, name="wp_scales", align_bytes=64)
+        results = [held.tile([P, T], F32, name=f"results{f}") for f in range(M // P)]
+
+        nc.gpsimd.memset(x_scales[:], 0)
+        for f in range(M // P):
+            nc.gpsimd.memset(results[f][:], 0.0)
+
+        x_raw, w_raw, w_grouped, w_quant, y, c_tiles, o, staged = {}, {}, {}, {}, {}, {}, {}, {}
+
+        def load_x(a, k):
+            lo, hi = X_CHUNKS[a][k]
+            raw = xstage.tile([P, PACK, hi - lo], F32, name=f"xraw{hi - lo}")
+            nc.sync.dma_start(out=raw[:], in_=xT[a * K_PASS:(a + 1) * K_PASS, lo:hi].rearrange("(p j) t -> p j t", j=PACK))
+            x_raw[a, k] = raw
+            if a == 0 and k == 0:
+                nc.sync.dma_start(offsets[:], offs)
+
+        def load_w(item):
+            e, a = divmod(item, PASSES)
+            raw = wstage.tile([P, PACK, N], F32, name="wraw")
+            nc.sync.dma_start(out=raw[:], in_=w[e, a * K_PASS:(a + 1) * K_PASS, :].rearrange("(p j) n -> p j n", j=PACK))
+            w_raw[item] = raw
+
+        def load_gate():
+            nc.sync.dma_start(out=gates[:], in_=gate[0:P, :])
+
+        def load_wp():
+            for b in range(4):
+                nc.sync.dma_start(
+                    out=wp_raw[b:P:4, :, :],
+                    in_=wp.rearrange("(h t b) f -> b h t f", t=PACK, b=4)[b],
+                )
+
+        def window(k):
+            experts = GATHERS[k]
+            return slice(experts[0] * C, (experts[-1] + 1) * C), slice(experts[0] * C // 16, (experts[-1] + 1) * C // 16)
+
+        def gather_words(a, k):
+            slots, cols = window(k)
+            nc.vector.tensor_copy(out=slot_codes[a][:, slots], in_=x_codes[a][:].indirect(offsets[:, cols]))
+
+        def gather_bytes(k):
+            slots, cols = window(k)
+            nc.vector.tensor_copy(out=slot_scales[:, slots], in_=x_scales[:].indirect(offsets[:, cols]))
+
+        def quantize_x(a):
+            grouped = xstage.tile([P, T * PACK], BF16, name="xgrouped", align_bytes=64)
+            for u, (lo, hi) in enumerate(X_UNITS):
+                k = [i for i, (l, h) in enumerate(X_CHUNKS[a]) if l <= lo and hi <= h][0]
+                base = X_CHUNKS[a][k][0]
+                copy_on(
+                    nc, X_ENGINES[a][u],
+                    grouped[:, PACK * lo:PACK * hi].rearrange("p (c i j) -> p c j i", i=4, j=PACK),
+                    x_raw[a, k][:, :, lo - base:hi - base].rearrange("p j (c i) -> p c j i", i=4),
+                )
+            for lo, hi in X_QUANTS:
+                nc.vector.quantize_mx(
+                    out=x_codes[a][:, lo:hi].bitcast(FP8X4),
+                    scales=x_scales[4 * a:P, lo:hi],
+                    in_=grouped[:, PACK * lo:PACK * hi],
+                )
+
+        def group_w(item):
+            grouped = wgroup.tile([P, N * PACK], BF16, name="wgrouped", align_bytes=64)
+            dst = grouped[:].rearrange("p (t h b j) -> p t h j b", t=4, b=4, j=PACK)
+            src = w_raw[item][:].rearrange("p j (h t b) -> p t h j b", t=4, b=4)
+            for t in range(4):
+                copy_on(nc, W_ENGINES[item][t], dst[:, t], src[:, t])
+            w_grouped[item] = grouped
+
+        def quantize_w(item):
+            codes = wcodes.tile([P, N], U32, name="w_codes", align_bytes=64)
+            scales = wcodes.tile([P, N], U8, name="w_scales", align_bytes=64)
+            step = N if Q_FULL[item] else N // 2
+            for lo in range(0, N, step):
+                nc.vector.quantize_mx(
+                    out=codes[:, lo:lo + step].bitcast(FP8X4),
+                    scales=scales[:, lo:lo + step],
+                    in_=w_grouped[item][:, PACK * lo:PACK * (lo + step)],
+                )
+            w_quant[item] = codes, scales
+
+        def quantize_wp():
+            copy_on(
+                nc, "S",
+                wp_grouped[:].rearrange("p (c i j) -> p c j i", i=4, j=PACK),
+                wp_raw[:].rearrange("p j (c i) -> p c j i", i=4),
+            )
+            for lo, hi in ((0, 256), (256, 384)):
+                nc.vector.quantize_mx(
+                    out=wp_codes[:, lo:hi].bitcast(FP8X4),
+                    scales=wp_scales[:, lo:hi],
+                    in_=wp_grouped[:, PACK * lo:PACK * hi],
+                )
+
+        def multiply(e):
+            for h in range(2):
+                slots = slice(e * C + h * HALF, e * C + (h + 1) * HALF)
+                acc = ypsum.tile([P, PACK, HALF], F32, name="y")
+                for t in range(PACK):
+                    for a in range(PASSES):
+                        codes, scales = w_quant[e * PASSES + a]
+                        nc.tensor.matmul_mx(
+                            out=acc[:, t, :],
+                            lhsT=codes[:, t * P:(t + 1) * P].bitcast(FP8X4),
+                            lhsT_scale=scales[:, t * P:(t + 1) * P],
+                            rhs=slot_codes[a][:, slots].bitcast(FP8X4),
+                            rhs_scale=slot_scales[4 * a:P, slots],
+                            start=(a == 0),
+                            stop=(a == PASSES - 1),
+                        )
+                y[e, h] = acc
+
+        def apply_gate(e):
+            grouped = small.tile([P, C * PACK], BF16, name="c_grouped", align_bytes=64)
+            for h in range(2):
+                slots = slice(e * C + h * HALF, e * C + (h + 1) * HALF)
+                nc.vector.tensor_tensor(
+                    grouped[:, PACK * h * HALF:PACK * (h + 1) * HALF].rearrange("p (u t) -> p u t", t=PACK),
+                    y[e, h][:].rearrange("p t u -> p u t"),
+                    gates[:, slots].unsqueeze(2).to_broadcast([P, HALF, PACK]),
+                    MULT,
+                )
+            c_tiles[e] = grouped
+
+        def project(e):
+            codes = small.tile([P, C], U32, name="c_codes", align_bytes=64)
+            scales = small.tile([P, C], U8, name="c_scales", align_bytes=64)
+            for h in range(2):
+                cols = slice(h * HALF, (h + 1) * HALF)
+                nc.vector.quantize_mx(
+                    out=codes[:, cols].bitcast(FP8X4),
+                    scales=scales[:, cols],
+                    in_=c_tiles[e][:, PACK * h * HALF:PACK * (h + 1) * HALF],
+                )
+                acc = opsum.tile([P, M // P, HALF], F32, name="o")
+                for f in range(M // P):
+                    nc.tensor.matmul_mx(
+                        out=acc[:, f, :],
+                        lhsT=wp_codes[:, f * P:(f + 1) * P].bitcast(FP8X4),
+                        lhsT_scale=wp_scales[:, f * P:(f + 1) * P],
+                        rhs=codes[:, cols].bitcast(FP8X4),
+                        rhs_scale=scales[:, cols],
+                        start=True,
+                        stop=True,
+                    )
+                o[e, h] = acc
+
+        def empty(e):
+            rows = small.tile([P, M // P, C], F32, name="staged")
+            for h in range(2):
+                dst = rows[:, :, h * HALF:(h + 1) * HALF]
+                if C_ENGINES[e][h] == "S":
+                    nc.scalar.copy(out=dst, in_=o[e, h][:])
+                else:
+                    nc.vector.tensor_copy(out=dst, in_=o[e, h][:])
+            staged[e] = rows
+
+        def scatter(e):
+            for f in range(M // P):
+                nc.vector.tensor_copy(
+                    out=results[f][:].indirect(offsets[:, e * C // 16:(e + 1) * C // 16]),
+                    in_=staged[e][:, f, :],
+                )
+
+        def store():
+            for f in range(M // P):
+                nc.sync.dma_start(out=out[f * P:(f + 1) * P, :], in_=results[f][:])
+
+        calls = {
+            "lx": load_x, "lw": load_w, "lg": load_gate, "lwp": load_wp, "gw": gather_words, "gb": gather_bytes,
+            "ix": quantize_x, "iw": group_w, "qw": quantize_w, "wpq": quantize_wp, "mm": multiply, "ga": apply_gate,
+            "qc": project, "cp": empty, "sc": scatter, "st": store,
+        }
+        for step in STEPS:
+            calls[step[0]](*step[1:])

@@ -23,17 +23,22 @@ PACK = 4
 K_PASS = P * PACK
 PASSES = K // K_PASS
 HALF = 128
-AHEAD = 6
+AHEAD = 4
+PAIRED = {2: 'turn_b', 5: 'turn_a', 8: 'turn_b', 11: 'turn_a'}
+STAGED = ('turn_a', 'turn_b', 'turn_a', 'turn_b')
+WP_ENGINE = 'S'
 WG = 6
 SMB = 2
 X_CHUNKS = (((0, 512), (512, 1280)), ((0, 512), (512, 1280)), ((0, 512), (512, 1280)))
 X_UNITS = ((0, 256), (256, 512), (512, 768), (768, 1024), (1024, 1280))
 X_QUANTS = ((0, 512), (512, 1024), (1024, 1280))
-X_ENGINES = ('SSVSV', 'VSVSS', 'SVVSV')
-W_ENGINES = ('SSSS', 'SSSS', 'SSSS', 'SSSV', 'SVSV', 'SVSV', 'SSSS', 'SSSS', 'SVSV', 'SSSS', 'SSSV', 'SSSS')
-Q_FULL = (False, False, True, True, False, False, False, True, True, True, True, False)
+X_ENGINES = ('VVVVS', 'SVSVS', 'SSSVS')
+W_ENGINES = ('SSSS', 'SSSV', 'SSSS', 'SSSV', 'SSSV', 'SSVV', 'SSSS', 'SSSS', 'SSSS', 'SSSS', 'SSSS', 'SSSS')
+Q_FULL = (True, True, True, False, False, True, True, False, False, True, True, True)
 C_ENGINES = ('SS', 'SS', 'SS', 'SS')
-GATHERS = ((0, 1), (2, 3))
+GATHERS = ((0,), (1, 2, 3))
+G_ON_POOL = ((False, False), (False, False), (False, False), (False, False))
+QC_FULL = (True, False, False, False)
 STEPS = (
     ('lx', 0, 0),
     ('lx', 0, 1),
@@ -53,20 +58,24 @@ STEPS = (
     ('iw', 0),
     ('qw', 0),
     ('lw', 6),
-    ('ix', 1),
-    ('ix', 2),
-    ('gw', 0, 0),
-    ('gw', 1, 0),
-    ('gw', 2, 0),
-    ('gb', 0),
-    ('wpq',),
     ('iw', 1),
     ('qw', 1),
     ('lw', 7),
+    ('wpq',),
+    ('gw', 0, 0),
+    ('ix', 1),
+    ('gw', 1, 0),
+    ('ix', 2),
+    ('gw', 2, 0),
+    ('gb', 1),
     ('iw', 2),
     ('qw', 2),
     ('lw', 8),
+    ('gb', 0),
+    ('gw', 2, 1),
     ('mm', 0),
+    ('gw', 0, 1),
+    ('gw', 1, 1),
     ('ga', 0),
     ('qc', 0),
     ('iw', 3),
@@ -75,40 +84,36 @@ STEPS = (
     ('iw', 4),
     ('qw', 4),
     ('lw', 10),
-    ('cp', 0),
     ('iw', 5),
     ('qw', 5),
-    ('lw', 11),
     ('mm', 1),
+    ('cp', 0),
+    ('sc', 0),
+    ('lw', 11),
     ('ga', 1),
     ('qc', 1),
-    ('gw', 0, 1),
-    ('gw', 1, 1),
-    ('gw', 2, 1),
-    ('gb', 1),
     ('iw', 6),
     ('qw', 6),
     ('iw', 7),
     ('qw', 7),
-    ('sc', 0),
     ('iw', 8),
     ('qw', 8),
     ('mm', 2),
+    ('cp', 1),
+    ('sc', 1),
     ('ga', 2),
     ('qc', 2),
     ('iw', 9),
     ('qw', 9),
     ('iw', 10),
     ('qw', 10),
-    ('cp', 1),
-    ('sc', 1),
     ('iw', 11),
     ('qw', 11),
     ('mm', 3),
-    ('ga', 3),
-    ('qc', 3),
     ('cp', 2),
     ('sc', 2),
+    ('ga', 3),
+    ('qc', 3),
     ('cp', 3),
     ('sc', 3),
     ('st',),
@@ -163,7 +168,10 @@ def tile_moe_nxt_lin_none_kernel(tc, xT, w, wp, gate, offs, out):
 
         def load_w(item):
             e, a = divmod(item, PASSES)
-            raw = wstage.tile([P, PACK, N], F32, name="wraw")
+            if item in PAIRED:
+                raw = wstage.tile([P, PACK, N], F32, name=f"wraw{item}", tag=PAIRED[item], bufs=1)
+            else:
+                raw = wstage.tile([P, PACK, N], F32, name="wraw")
             nc.sync.dma_start(out=raw[:], in_=w[e, a * K_PASS:(a + 1) * K_PASS, :].rearrange("(p j) n -> p j n", j=PACK))
             w_raw[item] = raw
 
@@ -228,7 +236,7 @@ def tile_moe_nxt_lin_none_kernel(tc, xT, w, wp, gate, offs, out):
 
         def quantize_wp():
             copy_on(
-                nc, "S",
+                nc, WP_ENGINE,
                 wp_grouped[:].rearrange("p (c i j) -> p c j i", i=4, j=PACK),
                 wp_raw[:].rearrange("p j (c i) -> p c j i", i=4),
             )
@@ -261,24 +269,28 @@ def tile_moe_nxt_lin_none_kernel(tc, xT, w, wp, gate, offs, out):
             grouped = small.tile([P, C * PACK], BF16, name="c_grouped", align_bytes=64)
             for h in range(2):
                 slots = slice(e * C + h * HALF, e * C + (h + 1) * HALF)
-                nc.vector.tensor_tensor(
-                    grouped[:, PACK * h * HALF:PACK * (h + 1) * HALF].rearrange("p (u t) -> p u t", t=PACK),
-                    y[e, h][:].rearrange("p t u -> p u t"),
-                    gates[:, slots].unsqueeze(2).to_broadcast([P, HALF, PACK]),
-                    MULT,
-                )
+                dst = grouped[:, PACK * h * HALF:PACK * (h + 1) * HALF].rearrange("p (u t) -> p u t", t=PACK)
+                factor = gates[:, slots].unsqueeze(2).to_broadcast([P, HALF, PACK])
+                if G_ON_POOL[e][h]:
+                    sums = small.tile([P, PACK, HALF], F32, name="sums")
+                    nc.scalar.copy(out=sums[:], in_=y[e, h][:])
+                    nc.gpsimd.tensor_tensor(dst, sums[:].rearrange("p t u -> p u t"), factor, MULT)
+                else:
+                    nc.vector.tensor_tensor(dst, y[e, h][:].rearrange("p t u -> p u t"), factor, MULT)
             c_tiles[e] = grouped
 
         def project(e):
             codes = small.tile([P, C], U32, name="c_codes", align_bytes=64)
             scales = small.tile([P, C], U8, name="c_scales", align_bytes=64)
+            step = C if QC_FULL[e] else HALF
+            for lo in range(0, C, step):
+                nc.vector.quantize_mx(
+                    out=codes[:, lo:lo + step].bitcast(FP8X4),
+                    scales=scales[:, lo:lo + step],
+                    in_=c_tiles[e][:, PACK * lo:PACK * (lo + step)],
+                )
             for h in range(2):
                 cols = slice(h * HALF, (h + 1) * HALF)
-                nc.vector.quantize_mx(
-                    out=codes[:, cols].bitcast(FP8X4),
-                    scales=scales[:, cols],
-                    in_=c_tiles[e][:, PACK * h * HALF:PACK * (h + 1) * HALF],
-                )
                 acc = opsum.tile([P, M // P, HALF], F32, name="o")
                 for f in range(M // P):
                     nc.tensor.matmul_mx(
@@ -293,7 +305,7 @@ def tile_moe_nxt_lin_none_kernel(tc, xT, w, wp, gate, offs, out):
                 o[e, h] = acc
 
         def empty(e):
-            rows = small.tile([P, M // P, C], F32, name="staged")
+            rows = wstage.tile([P, M // P, C], F32, name=f"staged{e}", tag=STAGED[e], bufs=1)
             for h in range(2):
                 dst = rows[:, :, h * HALF:(h + 1) * HALF]
                 if C_ENGINES[e][h] == "S":

@@ -1,6 +1,7 @@
 from contextlib import ExitStack
 
 import concourse.mybir as mybir
+from concourse.masks import make_identity
 
 K, T, E, C, N, M = 1536, 1280, 4, 256, 512, 384
 S = E * C
@@ -10,120 +11,138 @@ BYTES = 4 * (K * T + E * K * N + N * M + S + M * T) + 2 * S
 
 F32 = mybir.dt.float32
 BF16 = mybir.dt.bfloat16
+I32 = mybir.dt.int32
 U32 = mybir.dt.uint32
 U16 = mybir.dt.uint16
 U8 = mybir.dt.uint8
 FP8X4 = mybir.dt.float8_e4m3fn_x4
 COPY = mybir.ActivationFunctionType.Copy
 MULT = mybir.AluOpType.mult
-ADD = mybir.AluOpType.add
 
 P = 128
 PACK = 4
 K_PASS = P * PACK
 PASSES = K // K_PASS
 HALF = 128
+XBUFS = {256: 2, 512: 1, 768: 1, 1280: 2}
 AHEAD = 4
-PAIRED = {2: 'turn_b', 5: 'turn_a', 8: 'turn_b', 11: 'turn_a'}
+PAIRED = {2: 'turn_b', 5: 'turn_a', 8: 'turn_b', 10: 'turn_a'}
 STAGED = ('turn_a', 'turn_b', 'turn_a', 'turn_b')
-WP_ENGINE = 'S'
-WG = 6
+WP_ENGINE = 'V'
+WG = 5
 SMB = 2
-X_CHUNKS = (((0, 512), (512, 1280)), ((0, 512), (512, 1280)), ((0, 512), (512, 1280)))
-X_UNITS = ((0, 256), (256, 512), (512, 768), (768, 1024), (1024, 1280))
+X_CHUNKS = (((0, 512), (512, 1280)), ((0, 1280),), ((0, 1280),))
+X_UNITS = ((0, 512), (512, 1024), (1024, 1280))
 X_QUANTS = ((0, 512), (512, 1024), (1024, 1280))
-X_ENGINES = ('VVVVS', 'SVSVS', 'SSSVS')
-W_ENGINES = ('SSSS', 'SSSV', 'SSSS', 'SSSV', 'SSSV', 'SSVV', 'SSSS', 'SSSS', 'SSSS', 'SSSS', 'SSSS', 'SSSS')
-Q_FULL = (True, True, True, False, False, True, True, False, False, True, True, True)
-C_ENGINES = ('SS', 'SS', 'SS', 'SS')
-GATHERS = ((0,), (1, 2, 3))
-G_ON_POOL = ((False, False), (False, False), (False, False), (False, False))
-QC_FULL = (True, False, False, False)
+X_ENGINES = ('SVV', 'VVS', 'SVV')
+W_SHARES = ((('S', 512),), (('S', 256), ('V', 256)), (('S', 512),), (('S', 512),), (('S', 256), ('V', 256)), (('S', 512),), (('S', 256), ('V', 256)), (('S', 256), ('V', 256)), (('S', 512),), (('S', 512),), (('S', 512),), (('S', 512),))
+GATE_ENGINES = ('SV', 'VS', 'SS', 'SS')
+TURN_ENGINES = ('SS', 'SV', 'VV', 'SS')
+C_ENGINES = ('SS', 'SS', 'SS', 'SV')
+GATHERS = ((0,), (1,), (2, 3))
+QC_FULL = (False, True, False, False)
+WINDOW = 1280
 STEPS = (
     ('lx', 0, 0),
     ('lx', 0, 1),
     ('lx', 1, 0),
-    ('lx', 1, 1),
-    ('lx', 2, 0),
-    ('lx', 2, 1),
     ('lw', 0),
+    ('lx', 2, 0),
     ('lw', 1),
     ('lw', 2),
-    ('lg',),
-    ('lwp',),
     ('lw', 3),
+    ('lg',),
     ('lw', 4),
     ('lw', 5),
-    ('ix', 0),
+    ('lwp',),
     ('iw', 0),
     ('qw', 0),
     ('lw', 6),
+    ('ix', 0),
     ('iw', 1),
     ('qw', 1),
     ('lw', 7),
-    ('wpq',),
-    ('gw', 0, 0),
+    ('gw', 0, 1),
     ('ix', 1),
-    ('gw', 1, 0),
+    ('gw', 1, 1),
     ('ix', 2),
+    ('wpq',),
     ('gw', 2, 0),
-    ('gb', 1),
+    ('gb', 2),
     ('iw', 2),
     ('qw', 2),
     ('lw', 8),
+    ('gw', 0, 0),
+    ('gw', 1, 0),
     ('gb', 0),
-    ('gw', 2, 1),
-    ('mm', 0),
-    ('gw', 0, 1),
-    ('gw', 1, 1),
+    ('gb', 1),
+    ('m', 0, 0),
+    ('m', 0, 1),
+    ('m', 0, 2),
     ('ga', 0),
     ('qc', 0),
+    ('gw', 2, 1),
+    ('gw', 0, 2),
     ('iw', 3),
     ('qw', 3),
+    ('m', 1, 0),
     ('lw', 9),
+    ('gw', 1, 2),
+    ('gw', 2, 2),
     ('iw', 4),
     ('qw', 4),
-    ('lw', 10),
+    ('m', 1, 1),
+    ('lw', 11),
     ('iw', 5),
     ('qw', 5),
-    ('mm', 1),
+    ('m', 1, 2),
     ('cp', 0),
-    ('sc', 0),
-    ('lw', 11),
     ('ga', 1),
     ('qc', 1),
+    ('sc', 0, 0),
+    ('sc', 0, 1),
+    ('sc', 0, 2),
+    ('lw', 10),
     ('iw', 6),
     ('qw', 6),
+    ('m', 2, 0),
     ('iw', 7),
     ('qw', 7),
+    ('m', 2, 1),
     ('iw', 8),
     ('qw', 8),
-    ('mm', 2),
+    ('m', 2, 2),
     ('cp', 1),
-    ('sc', 1),
     ('ga', 2),
+    ('sc', 1, 0),
+    ('sc', 1, 1),
+    ('sc', 1, 2),
     ('qc', 2),
     ('iw', 9),
     ('qw', 9),
+    ('m', 3, 0),
     ('iw', 10),
     ('qw', 10),
+    ('m', 3, 1),
+    ('cp', 2),
     ('iw', 11),
     ('qw', 11),
-    ('mm', 3),
-    ('cp', 2),
-    ('sc', 2),
+    ('m', 3, 2),
+    ('sc', 2, 0),
+    ('sc', 2, 1),
+    ('sc', 2, 2),
     ('ga', 3),
     ('qc', 3),
     ('cp', 3),
-    ('sc', 3),
+    ('sc', 3, 0),
+    ('sc', 3, 1),
+    ('sc', 3, 2),
     ('st',),
 )
 
 def copy_on(nc, engine, out, in_):
     if engine == "S":
         nc.scalar.activation(out=out, in_=in_, func=COPY)
-    elif engine == "P":
-        nc.gpsimd.tensor_scalar(out=out, in0=in_, scalar1=1.0, scalar2=0.0, op0=MULT, op1=ADD)
     else:
         nc.vector.tensor_copy(out=out, in_=in_)
 
@@ -135,15 +154,18 @@ def tile_moe_nxt_lin_none_kernel(tc, xT, w, wp, gate, offs, out):
         xstage = ctx.enter_context(tc.tile_pool(name="xstage", bufs=2))
         wstage = ctx.enter_context(tc.tile_pool(name="wstage", bufs=AHEAD))
         wgroup = ctx.enter_context(tc.tile_pool(name="wgroup", bufs=WG))
-        wcodes = ctx.enter_context(tc.tile_pool(name="wcodes", bufs=E * PASSES))
+        wcodes = ctx.enter_context(tc.tile_pool(name="wcodes", bufs=8))
         small = ctx.enter_context(tc.tile_pool(name="small", bufs=SMB))
         ypsum = ctx.enter_context(tc.psum_pool(name="ypsum", bufs=4))
-        opsum = ctx.enter_context(tc.psum_pool(name="opsum", bufs=4))
+        tpsum = ctx.enter_context(tc.psum_pool(name="tpsum", bufs=2))
+        opsum = ctx.enter_context(tc.psum_pool(name="opsum", bufs=2))
 
         offsets = held.tile([P, S // 16], U16, name="offsets")
-        gates = held.tile([P, S], F32, name="gates")
-        x_codes = [held.tile([P, T], U32, name=f"x_codes{a}", align_bytes=64) for a in range(PASSES)]
-        x_scales = held.tile([P, T], U8, name="x_scales", align_bytes=64)
+        identity = held.tile([P, P], F32, name="identity")
+        gate_rows = held.tile([P, P], F32, name="gate_rows")
+        gate_cols = held.tile([P, S // P], F32, name="gate_cols")
+        x_codes = [held.tile([P, WINDOW], I32, name=f"x_codes{a}", align_bytes=64) for a in range(PASSES)]
+        x_scales = held.tile([P, WINDOW], U8, name="x_scales", align_bytes=64)
         slot_codes = [held.tile([P, S], U32, name=f"slot_codes{a}", align_bytes=64) for a in range(PASSES)]
         slot_scales = held.tile([P, S], U8, name="slot_scales", align_bytes=64)
         wp_raw = held.tile([P, PACK, M], F32, name="wp_raw")
@@ -153,6 +175,11 @@ def tile_moe_nxt_lin_none_kernel(tc, xT, w, wp, gate, offs, out):
         results = [held.tile([P, T], F32, name=f"results{f}") for f in range(M // P)]
 
         nc.gpsimd.memset(x_scales[:], 0)
+        nc.gpsimd.memset(gate_rows[:], 0.0)
+        make_identity(nc, identity[:])
+        for a in range(PASSES):
+            if WINDOW > T:
+                nc.vector.memset(x_codes[a][:, T:WINDOW], 0)
         for f in range(M // P):
             nc.gpsimd.memset(results[f][:], 0.0)
 
@@ -160,7 +187,7 @@ def tile_moe_nxt_lin_none_kernel(tc, xT, w, wp, gate, offs, out):
 
         def load_x(a, k):
             lo, hi = X_CHUNKS[a][k]
-            raw = xstage.tile([P, PACK, hi - lo], F32, name=f"xraw{hi - lo}")
+            raw = xstage.tile([P, PACK, hi - lo], F32, name=f"xraw{hi - lo}", bufs=XBUFS[hi - lo])
             nc.sync.dma_start(out=raw[:], in_=xT[a * K_PASS:(a + 1) * K_PASS, lo:hi].rearrange("(p j) t -> p j t", j=PACK))
             x_raw[a, k] = raw
             if a == 0 and k == 0:
@@ -176,14 +203,13 @@ def tile_moe_nxt_lin_none_kernel(tc, xT, w, wp, gate, offs, out):
             w_raw[item] = raw
 
         def load_gate():
-            nc.sync.dma_start(out=gates[:], in_=gate[0:P, :])
+            nc.sync.dma_start(out=gate_rows[0:S // P, :], in_=gate[0].rearrange("(s u) -> s u", u=P))
+            turned = tpsum.tile([P, 2, P], F32, name="turned")
+            nc.tensor.transpose(turned[:, 0, :], gate_rows[:], identity[:])
+            nc.vector.tensor_copy(out=gate_cols[:], in_=turned[:, 0, 0:S // P])
 
         def load_wp():
-            for b in range(4):
-                nc.sync.dma_start(
-                    out=wp_raw[b:P:4, :, :],
-                    in_=wp.rearrange("(h t b) f -> b h t f", t=PACK, b=4)[b],
-                )
+            nc.sync.dma_start(out=wp_raw[:], in_=wp.rearrange("(p j) f -> p j f", j=PACK))
 
         def window(k):
             experts = GATHERS[k]
@@ -191,7 +217,7 @@ def tile_moe_nxt_lin_none_kernel(tc, xT, w, wp, gate, offs, out):
 
         def gather_words(a, k):
             slots, cols = window(k)
-            nc.vector.tensor_copy(out=slot_codes[a][:, slots], in_=x_codes[a][:].indirect(offsets[:, cols]))
+            nc.vector.tensor_copy(out=slot_codes[a][:, slots], in_=x_codes[a][:].bitcast(U32).indirect(offsets[:, cols]))
 
         def gather_bytes(k):
             slots, cols = window(k)
@@ -216,22 +242,21 @@ def tile_moe_nxt_lin_none_kernel(tc, xT, w, wp, gate, offs, out):
 
         def group_w(item):
             grouped = wgroup.tile([P, N * PACK], BF16, name="wgrouped", align_bytes=64)
-            dst = grouped[:].rearrange("p (t h b j) -> p t h j b", t=4, b=4, j=PACK)
-            src = w_raw[item][:].rearrange("p j (h t b) -> p t h j b", t=4, b=4)
-            for t in range(4):
-                copy_on(nc, W_ENGINES[item][t], dst[:, t], src[:, t])
+            lo = 0
+            for engine, width in W_SHARES[item]:
+                hi = lo + width
+                copy_on(
+                    nc, engine,
+                    grouped[:, PACK * lo:PACK * hi].rearrange("p (c i j) -> p c j i", i=4, j=PACK),
+                    w_raw[item][:, :, lo:hi].rearrange("p j (c i) -> p c j i", i=4),
+                )
+                lo = hi
             w_grouped[item] = grouped
 
         def quantize_w(item):
             codes = wcodes.tile([P, N], U32, name="w_codes", align_bytes=64)
             scales = wcodes.tile([P, N], U8, name="w_scales", align_bytes=64)
-            step = N if Q_FULL[item] else N // 2
-            for lo in range(0, N, step):
-                nc.vector.quantize_mx(
-                    out=codes[:, lo:lo + step].bitcast(FP8X4),
-                    scales=scales[:, lo:lo + step],
-                    in_=w_grouped[item][:, PACK * lo:PACK * (lo + step)],
-                )
+            nc.vector.quantize_mx(out=codes[:].bitcast(FP8X4), scales=scales[:], in_=w_grouped[item][:])
             w_quant[item] = codes, scales
 
         def quantize_wp():
@@ -247,36 +272,43 @@ def tile_moe_nxt_lin_none_kernel(tc, xT, w, wp, gate, offs, out):
                     in_=wp_grouped[:, PACK * lo:PACK * hi],
                 )
 
-        def multiply(e):
+        def multiply(e, a):
+            codes, scales = w_quant[e * PASSES + a]
             for h in range(2):
+                if a == 0:
+                    y[e, h] = ypsum.tile([P, N], F32, name="y")
                 slots = slice(e * C + h * HALF, e * C + (h + 1) * HALF)
-                acc = ypsum.tile([P, PACK, HALF], F32, name="y")
-                for t in range(PACK):
-                    for a in range(PASSES):
-                        codes, scales = w_quant[e * PASSES + a]
-                        nc.tensor.matmul_mx(
-                            out=acc[:, t, :],
-                            lhsT=codes[:, t * P:(t + 1) * P].bitcast(FP8X4),
-                            lhsT_scale=scales[:, t * P:(t + 1) * P],
-                            rhs=slot_codes[a][:, slots].bitcast(FP8X4),
-                            rhs_scale=slot_scales[4 * a:P, slots],
-                            start=(a == 0),
-                            stop=(a == PASSES - 1),
-                        )
-                y[e, h] = acc
+                nc.tensor.matmul_mx(
+                    out=y[e, h][:],
+                    lhsT=slot_codes[a][:, slots].bitcast(FP8X4),
+                    lhsT_scale=slot_scales[4 * a:P, slots],
+                    rhs=codes[:].bitcast(FP8X4),
+                    rhs_scale=scales[:],
+                    start=(a == 0),
+                    stop=(a == PASSES - 1),
+                )
 
         def apply_gate(e):
             grouped = small.tile([P, C * PACK], BF16, name="c_grouped", align_bytes=64)
             for h in range(2):
-                slots = slice(e * C + h * HALF, e * C + (h + 1) * HALF)
-                dst = grouped[:, PACK * h * HALF:PACK * (h + 1) * HALF].rearrange("p (u t) -> p u t", t=PACK)
-                factor = gates[:, slots].unsqueeze(2).to_broadcast([P, HALF, PACK])
-                if G_ON_POOL[e][h]:
-                    sums = small.tile([P, PACK, HALF], F32, name="sums")
-                    nc.scalar.copy(out=sums[:], in_=y[e, h][:])
-                    nc.gpsimd.tensor_tensor(dst, sums[:].rearrange("p t u -> p u t"), factor, MULT)
+                column = gate_cols[:, 2 * e + h:2 * e + h + 1]
+                rows = small.tile([P, N], BF16, name="c_rows", bufs=3)
+                dst = rows[:].rearrange("s (u p e) -> s u p e", u=2, e=2)
+                src = y[e, h][:].rearrange("s (p u e) -> s u p e", u=2, e=2)
+                if GATE_ENGINES[e][h] == "S":
+                    nc.scalar.activation(out=dst, in_=src, func=COPY, scale=column)
                 else:
-                    nc.vector.tensor_tensor(dst, y[e, h][:].rearrange("p t u -> p u t"), factor, MULT)
+                    nc.vector.tensor_scalar(out=dst, in0=src, scalar1=column, scalar2=None, op0=MULT)
+                words = rows[:].bitcast(F32)
+                turned = tpsum.tile([P, 2, P], F32, name="turned")
+                for u in range(2):
+                    nc.tensor.transpose(turned[:, u, :], words[:, u * P:(u + 1) * P], identity[:])
+                dst = grouped[:, PACK * h * HALF:PACK * (h + 1) * HALF].bitcast(F32).rearrange("p (r u) -> p r u", u=2)
+                src = turned[:].rearrange("p u r -> p r u")
+                if TURN_ENGINES[e][h] == "S":
+                    nc.scalar.copy(out=dst, in_=src)
+                else:
+                    nc.vector.tensor_copy(out=dst, in_=src)
             c_tiles[e] = grouped
 
         def project(e):
@@ -314,12 +346,11 @@ def tile_moe_nxt_lin_none_kernel(tc, xT, w, wp, gate, offs, out):
                     nc.vector.tensor_copy(out=dst, in_=o[e, h][:])
             staged[e] = rows
 
-        def scatter(e):
-            for f in range(M // P):
-                nc.vector.tensor_copy(
-                    out=results[f][:].indirect(offsets[:, e * C // 16:(e + 1) * C // 16]),
-                    in_=staged[e][:, f, :],
-                )
+        def scatter(e, f):
+            nc.vector.tensor_copy(
+                out=results[f][:].indirect(offsets[:, e * C // 16:(e + 1) * C // 16]),
+                in_=staged[e][:, f, :],
+            )
 
         def store():
             for f in range(M // P):
@@ -327,7 +358,7 @@ def tile_moe_nxt_lin_none_kernel(tc, xT, w, wp, gate, offs, out):
 
         calls = {
             "lx": load_x, "lw": load_w, "lg": load_gate, "lwp": load_wp, "gw": gather_words, "gb": gather_bytes,
-            "ix": quantize_x, "iw": group_w, "qw": quantize_w, "wpq": quantize_wp, "mm": multiply, "ga": apply_gate,
+            "ix": quantize_x, "iw": group_w, "qw": quantize_w, "wpq": quantize_wp, "m": multiply, "ga": apply_gate,
             "qc": project, "cp": empty, "sc": scatter, "st": store,
         }
         for step in STEPS:

from contextlib import ExitStack

import concourse.mybir as mybir
from concourse.masks import make_identity

K, T, E, C, N, M = 1536, 1280, 4, 256, 512, 384
S = E * C

FLOPS = 2 * S * K * N + 2 * S * N * M
BYTES = 4 * (K * T + E * K * N + N * M + S + M * T) + 2 * S

F32 = mybir.dt.float32
BF16 = mybir.dt.bfloat16
I32 = mybir.dt.int32
U32 = mybir.dt.uint32
U16 = mybir.dt.uint16
U8 = mybir.dt.uint8
FP8X4 = mybir.dt.float8_e4m3fn_x4
COPY = mybir.ActivationFunctionType.Copy
MULT = mybir.AluOpType.mult

P = 128
PACK = 4
K_PASS = P * PACK
PASSES = K // K_PASS
HALF = 128
XBUFS = {256: 2, 512: 1, 768: 1, 1280: 2}
AHEAD = 4
PAIRED = {2: 'turn_b', 5: 'turn_a', 8: 'turn_b', 10: 'turn_a'}
STAGED = ('turn_a', 'turn_b', 'turn_a', 'turn_b')
WP_ENGINE = 'V'
WG = 5
SMB = 2
X_CHUNKS = (((0, 512), (512, 1280)), ((0, 1280),), ((0, 1280),))
X_UNITS = ((0, 512), (512, 1024), (1024, 1280))
X_QUANTS = ((0, 512), (512, 1024), (1024, 1280))
X_ENGINES = ('SVV', 'VVS', 'SVV')
W_SHARES = ((('S', 512),), (('S', 256), ('V', 256)), (('S', 512),), (('S', 512),), (('S', 256), ('V', 256)), (('S', 512),), (('S', 256), ('V', 256)), (('S', 256), ('V', 256)), (('S', 512),), (('S', 512),), (('S', 512),), (('S', 512),))
GATE_ENGINES = ('SV', 'VS', 'SS', 'SS')
TURN_ENGINES = ('SS', 'SV', 'VV', 'SS')
C_ENGINES = ('SS', 'SS', 'SS', 'SV')
GATHERS = ((0,), (1,), (2, 3))
QC_FULL = (False, True, False, False)
WINDOW = 1280
STEPS = (
    ('lx', 0, 0),
    ('lx', 0, 1),
    ('lx', 1, 0),
    ('lw', 0),
    ('lx', 2, 0),
    ('lw', 1),
    ('lw', 2),
    ('lw', 3),
    ('lg',),
    ('lw', 4),
    ('lw', 5),
    ('lwp',),
    ('iw', 0),
    ('qw', 0),
    ('lw', 6),
    ('ix', 0),
    ('iw', 1),
    ('qw', 1),
    ('lw', 7),
    ('gw', 0, 1),
    ('ix', 1),
    ('gw', 1, 1),
    ('ix', 2),
    ('wpq',),
    ('gw', 2, 0),
    ('gb', 2),
    ('iw', 2),
    ('qw', 2),
    ('lw', 8),
    ('gw', 0, 0),
    ('gw', 1, 0),
    ('gb', 0),
    ('gb', 1),
    ('m', 0, 0),
    ('m', 0, 1),
    ('m', 0, 2),
    ('ga', 0),
    ('qc', 0),
    ('gw', 2, 1),
    ('gw', 0, 2),
    ('iw', 3),
    ('qw', 3),
    ('m', 1, 0),
    ('lw', 9),
    ('gw', 1, 2),
    ('gw', 2, 2),
    ('iw', 4),
    ('qw', 4),
    ('m', 1, 1),
    ('lw', 11),
    ('iw', 5),
    ('qw', 5),
    ('m', 1, 2),
    ('cp', 0),
    ('ga', 1),
    ('qc', 1),
    ('sc', 0, 0),
    ('sc', 0, 1),
    ('sc', 0, 2),
    ('lw', 10),
    ('iw', 6),
    ('qw', 6),
    ('m', 2, 0),
    ('iw', 7),
    ('qw', 7),
    ('m', 2, 1),
    ('iw', 8),
    ('qw', 8),
    ('m', 2, 2),
    ('cp', 1),
    ('ga', 2),
    ('sc', 1, 0),
    ('sc', 1, 1),
    ('sc', 1, 2),
    ('qc', 2),
    ('iw', 9),
    ('qw', 9),
    ('m', 3, 0),
    ('iw', 10),
    ('qw', 10),
    ('m', 3, 1),
    ('cp', 2),
    ('iw', 11),
    ('qw', 11),
    ('m', 3, 2),
    ('sc', 2, 0),
    ('sc', 2, 1),
    ('sc', 2, 2),
    ('ga', 3),
    ('qc', 3),
    ('cp', 3),
    ('sc', 3, 0),
    ('sc', 3, 1),
    ('sc', 3, 2),
    ('st',),
)

def copy_on(nc, engine, out, in_):
    if engine == "S":
        nc.scalar.activation(out=out, in_=in_, func=COPY)
    else:
        nc.vector.tensor_copy(out=out, in_=in_)


def tile_moe_nxt_lin_none_kernel(tc, xT, w, wp, gate, offs, out):
    nc = tc.nc
    with ExitStack() as ctx:
        held = ctx.enter_context(tc.tile_pool(name="held", bufs=1))
        xstage = ctx.enter_context(tc.tile_pool(name="xstage", bufs=2))
        wstage = ctx.enter_context(tc.tile_pool(name="wstage", bufs=AHEAD))
        wgroup = ctx.enter_context(tc.tile_pool(name="wgroup", bufs=WG))
        wcodes = ctx.enter_context(tc.tile_pool(name="wcodes", bufs=8))
        small = ctx.enter_context(tc.tile_pool(name="small", bufs=SMB))
        ypsum = ctx.enter_context(tc.psum_pool(name="ypsum", bufs=4))
        tpsum = ctx.enter_context(tc.psum_pool(name="tpsum", bufs=2))
        opsum = ctx.enter_context(tc.psum_pool(name="opsum", bufs=2))

        offsets = held.tile([P, S // 16], U16, name="offsets")
        identity = held.tile([P, P], F32, name="identity")
        gate_rows = held.tile([P, P], F32, name="gate_rows")
        gate_cols = held.tile([P, S // P], F32, name="gate_cols")
        x_codes = [held.tile([P, WINDOW], I32, name=f"x_codes{a}", align_bytes=64) for a in range(PASSES)]
        x_scales = held.tile([P, WINDOW], U8, name="x_scales", align_bytes=64)
        slot_codes = [held.tile([P, S], U32, name=f"slot_codes{a}", align_bytes=64) for a in range(PASSES)]
        slot_scales = held.tile([P, S], U8, name="slot_scales", align_bytes=64)
        wp_raw = held.tile([P, PACK, M], F32, name="wp_raw")
        wp_grouped = held.tile([P, M * PACK], BF16, name="wp_grouped", align_bytes=64)
        wp_codes = held.tile([P, M], U32, name="wp_codes", align_bytes=64)
        wp_scales = held.tile([P, M], U8, name="wp_scales", align_bytes=64)
        results = [held.tile([P, T], F32, name=f"results{f}") for f in range(M // P)]

        nc.gpsimd.memset(x_scales[:], 0)
        nc.gpsimd.memset(gate_rows[:], 0.0)
        make_identity(nc, identity[:])
        for a in range(PASSES):
            if WINDOW > T:
                nc.vector.memset(x_codes[a][:, T:WINDOW], 0)
        for f in range(M // P):
            nc.gpsimd.memset(results[f][:], 0.0)

        x_raw, w_raw, w_grouped, w_quant, y, c_tiles, o, staged = {}, {}, {}, {}, {}, {}, {}, {}

        def load_x(a, k):
            lo, hi = X_CHUNKS[a][k]
            raw = xstage.tile([P, PACK, hi - lo], F32, name=f"xraw{hi - lo}", bufs=XBUFS[hi - lo])
            nc.sync.dma_start(out=raw[:], in_=xT[a * K_PASS:(a + 1) * K_PASS, lo:hi].rearrange("(p j) t -> p j t", j=PACK))
            x_raw[a, k] = raw
            if a == 0 and k == 0:
                nc.sync.dma_start(offsets[:], offs)

        def load_w(item):
            e, a = divmod(item, PASSES)
            if item in PAIRED:
                raw = wstage.tile([P, PACK, N], F32, name=f"wraw{item}", tag=PAIRED[item], bufs=1)
            else:
                raw = wstage.tile([P, PACK, N], F32, name="wraw")
            nc.sync.dma_start(out=raw[:], in_=w[e, a * K_PASS:(a + 1) * K_PASS, :].rearrange("(p j) n -> p j n", j=PACK))
            w_raw[item] = raw

        def load_gate():
            nc.sync.dma_start(out=gate_rows[0:S // P, :], in_=gate[0].rearrange("(s u) -> s u", u=P))
            turned = tpsum.tile([P, 2, P], F32, name="turned")
            nc.tensor.transpose(turned[:, 0, :], gate_rows[:], identity[:])
            nc.vector.tensor_copy(out=gate_cols[:], in_=turned[:, 0, 0:S // P])

        def load_wp():
            nc.sync.dma_start(out=wp_raw[:], in_=wp.rearrange("(p j) f -> p j f", j=PACK))

        def window(k):
            experts = GATHERS[k]
            return slice(experts[0] * C, (experts[-1] + 1) * C), slice(experts[0] * C // 16, (experts[-1] + 1) * C // 16)

        def gather_words(a, k):
            slots, cols = window(k)
            nc.vector.tensor_copy(out=slot_codes[a][:, slots], in_=x_codes[a][:].bitcast(U32).indirect(offsets[:, cols]))

        def gather_bytes(k):
            slots, cols = window(k)
            nc.vector.tensor_copy(out=slot_scales[:, slots], in_=x_scales[:].indirect(offsets[:, cols]))

        def quantize_x(a):
            grouped = xstage.tile([P, T * PACK], BF16, name="xgrouped", align_bytes=64)
            for u, (lo, hi) in enumerate(X_UNITS):
                k = [i for i, (l, h) in enumerate(X_CHUNKS[a]) if l <= lo and hi <= h][0]
                base = X_CHUNKS[a][k][0]
                copy_on(
                    nc, X_ENGINES[a][u],
                    grouped[:, PACK * lo:PACK * hi].rearrange("p (c i j) -> p c j i", i=4, j=PACK),
                    x_raw[a, k][:, :, lo - base:hi - base].rearrange("p j (c i) -> p c j i", i=4),
                )
            for lo, hi in X_QUANTS:
                nc.vector.quantize_mx(
                    out=x_codes[a][:, lo:hi].bitcast(FP8X4),
                    scales=x_scales[4 * a:P, lo:hi],
                    in_=grouped[:, PACK * lo:PACK * hi],
                )

        def group_w(item):
            grouped = wgroup.tile([P, N * PACK], BF16, name="wgrouped", align_bytes=64)
            lo = 0
            for engine, width in W_SHARES[item]:
                hi = lo + width
                copy_on(
                    nc, engine,
                    grouped[:, PACK * lo:PACK * hi].rearrange("p (c i j) -> p c j i", i=4, j=PACK),
                    w_raw[item][:, :, lo:hi].rearrange("p j (c i) -> p c j i", i=4),
                )
                lo = hi
            w_grouped[item] = grouped

        def quantize_w(item):
            codes = wcodes.tile([P, N], U32, name="w_codes", align_bytes=64)
            scales = wcodes.tile([P, N], U8, name="w_scales", align_bytes=64)
            nc.vector.quantize_mx(out=codes[:].bitcast(FP8X4), scales=scales[:], in_=w_grouped[item][:])
            w_quant[item] = codes, scales

        def quantize_wp():
            copy_on(
                nc, WP_ENGINE,
                wp_grouped[:].rearrange("p (c i j) -> p c j i", i=4, j=PACK),
                wp_raw[:].rearrange("p j (c i) -> p c j i", i=4),
            )
            for lo, hi in ((0, 256), (256, 384)):
                nc.vector.quantize_mx(
                    out=wp_codes[:, lo:hi].bitcast(FP8X4),
                    scales=wp_scales[:, lo:hi],
                    in_=wp_grouped[:, PACK * lo:PACK * hi],
                )

        def multiply(e, a):
            codes, scales = w_quant[e * PASSES + a]
            for h in range(2):
                if a == 0:
                    y[e, h] = ypsum.tile([P, N], F32, name="y")
                slots = slice(e * C + h * HALF, e * C + (h + 1) * HALF)
                nc.tensor.matmul_mx(
                    out=y[e, h][:],
                    lhsT=slot_codes[a][:, slots].bitcast(FP8X4),
                    lhsT_scale=slot_scales[4 * a:P, slots],
                    rhs=codes[:].bitcast(FP8X4),
                    rhs_scale=scales[:],
                    start=(a == 0),
                    stop=(a == PASSES - 1),
                )

        def apply_gate(e):
            grouped = small.tile([P, C * PACK], BF16, name="c_grouped", align_bytes=64)
            for h in range(2):
                column = gate_cols[:, 2 * e + h:2 * e + h + 1]
                rows = small.tile([P, N], BF16, name="c_rows", bufs=3)
                dst = rows[:].rearrange("s (u p e) -> s u p e", u=2, e=2)
                src = y[e, h][:].rearrange("s (p u e) -> s u p e", u=2, e=2)
                if GATE_ENGINES[e][h] == "S":
                    nc.scalar.activation(out=dst, in_=src, func=COPY, scale=column)
                else:
                    nc.vector.tensor_scalar(out=dst, in0=src, scalar1=column, scalar2=None, op0=MULT)
                words = rows[:].bitcast(F32)
                turned = tpsum.tile([P, 2, P], F32, name="turned")
                for u in range(2):
                    nc.tensor.transpose(turned[:, u, :], words[:, u * P:(u + 1) * P], identity[:])
                dst = grouped[:, PACK * h * HALF:PACK * (h + 1) * HALF].bitcast(F32).rearrange("p (r u) -> p r u", u=2)
                src = turned[:].rearrange("p u r -> p r u")
                if TURN_ENGINES[e][h] == "S":
                    nc.scalar.copy(out=dst, in_=src)
                else:
                    nc.vector.tensor_copy(out=dst, in_=src)
            c_tiles[e] = grouped

        def project(e):
            codes = small.tile([P, C], U32, name="c_codes", align_bytes=64)
            scales = small.tile([P, C], U8, name="c_scales", align_bytes=64)
            step = C if QC_FULL[e] else HALF
            for lo in range(0, C, step):
                nc.vector.quantize_mx(
                    out=codes[:, lo:lo + step].bitcast(FP8X4),
                    scales=scales[:, lo:lo + step],
                    in_=c_tiles[e][:, PACK * lo:PACK * (lo + step)],
                )
            for h in range(2):
                cols = slice(h * HALF, (h + 1) * HALF)
                acc = opsum.tile([P, M // P, HALF], F32, name="o")
                for f in range(M // P):
                    nc.tensor.matmul_mx(
                        out=acc[:, f, :],
                        lhsT=wp_codes[:, f * P:(f + 1) * P].bitcast(FP8X4),
                        lhsT_scale=wp_scales[:, f * P:(f + 1) * P],
                        rhs=codes[:, cols].bitcast(FP8X4),
                        rhs_scale=scales[:, cols],
                        start=True,
                        stop=True,
                    )
                o[e, h] = acc

        def empty(e):
            rows = wstage.tile([P, M // P, C], F32, name=f"staged{e}", tag=STAGED[e], bufs=1)
            for h in range(2):
                dst = rows[:, :, h * HALF:(h + 1) * HALF]
                if C_ENGINES[e][h] == "S":
                    nc.scalar.copy(out=dst, in_=o[e, h][:])
                else:
                    nc.vector.tensor_copy(out=dst, in_=o[e, h][:])
            staged[e] = rows

        def scatter(e, f):
            nc.vector.tensor_copy(
                out=results[f][:].indirect(offsets[:, e * C // 16:(e + 1) * C // 16]),
                in_=staged[e][:, f, :],
            )

        def store():
            for f in range(M // P):
                nc.sync.dma_start(out=out[f * P:(f + 1) * P, :], in_=results[f][:])

        calls = {
            "lx": load_x, "lw": load_w, "lg": load_gate, "lwp": load_wp, "gw": gather_words, "gb": gather_bytes,
            "ix": quantize_x, "iw": group_w, "qw": quantize_w, "wpq": quantize_wp, "m": multiply, "ga": apply_gate,
            "qc": project, "cp": empty, "sc": scatter, "st": store,
        }
        for step in STEPS:
            calls[step[0]](*step[1:])
